import numpy as np
import ml_dtypes


def mxq(x, axis, fmt="e4m3"):
    dtype, down = {"e4m3": (ml_dtypes.float8_e4m3fn, 7), "e5m2": (ml_dtypes.float8_e5m2, 14)}[fmt]
    v = np.moveaxis(np.asarray(x, np.float32).astype(ml_dtypes.bfloat16).astype(np.float64), axis, -1)
    blocks = v.reshape(v.shape[:-1] + (-1, 32))
    amax = np.abs(blocks).max(-1, keepdims=True)
    byte = np.maximum(np.where(amax > 0, np.frexp(amax)[1] - 1 + 127, 0) - down, 1)
    scale = np.exp2(byte - 127.0)
    codes = (blocks / scale).astype(np.float32).astype(dtype).astype(np.float64)
    return np.moveaxis((codes * scale).reshape(v.shape), -1, axis)


WIDE = False


def mx_kscale(k):
    if not WIDE:
        return np.ones(k)
    levels = np.array([30, -30])
    if k % 512:
        return np.exp2(np.random.permutation(np.resize(levels, k // 32))).repeat(32)
    a = np.empty((k // 512, 16))
    for p in range(k // 512):
        a[p, :8] = np.random.permutation(np.resize(levels, 8))
        for g in range(8):
            far = levels[np.abs(levels - a[p, g]) >= 10]
            a[p, g + 8] = far[np.random.randint(len(far))]
    return np.exp2(a.ravel()).repeat(32)


def f64(x):
    return np.asarray(x).astype(np.float64)


def striped(idx):
    return np.tile(np.asarray(idx).reshape(-1, 16).T, (8, 1)).astype(np.uint16)


def unstriped(offs):
    return offs[:16].T.reshape(-1).astype(np.int64)


E2M1 = np.array([0.0, 0.5, 1.0, 1.5, 2.0, 3.0, 4.0, 6.0, -0.0, -0.5, -1.0, -1.5, -2.0, -3.0, -4.0, -6.0])


def pack_weight(w, fmt):
    k, n = w.shape
    w = f64(np.asarray(w, np.float32).astype(ml_dtypes.bfloat16)).reshape(k // 32, 32, n)
    amax = np.abs(w).max(1)
    if fmt in ("e4m3", "e5m2"):
        byte = np.frexp(amax)[1] - 1 + 127 - (7 if fmt == "e4m3" else 14)
    else:
        mant, ex = np.frexp(amax / 6.0)
        byte = np.where(mant > 0.5, ex, ex - 1) + 127
    byte = np.clip(np.where(amax > 0, byte, 1), 1, 254)
    scaled = (w * np.exp2(127.0 - byte)[:, None, :]).reshape(k, n).astype(np.float32)
    by_word = np.ascontiguousarray(scaled.reshape(k // 512, 128, 4, n).transpose(0, 1, 3, 2))
    if fmt in ("e4m3", "e5m2"):
        words = by_word.astype(ml_dtypes.float8_e4m3fn if fmt == "e4m3" else ml_dtypes.float8_e5m2).view(np.uint8)
    else:
        c = by_word.astype(ml_dtypes.float4_e2m1fn).view(np.uint8) & 0xF
        words = (c[..., 0::2] | (c[..., 1::2] << 4)).reshape(k // 512, 128, 2 * n)
    return np.ascontiguousarray(words), np.ascontiguousarray(byte.astype(np.uint8).reshape(k // 512, 16, n))


def unpack_weight(words, scales, fmt):
    g, _, n = scales.shape
    words = np.ascontiguousarray(words).reshape(g, 128, n, -1)
    if fmt in ("e4m3", "e5m2"):
        vals = words.view(ml_dtypes.float8_e4m3fn if fmt == "e4m3" else ml_dtypes.float8_e5m2).astype(np.float64)
    else:
        nib = np.empty((g, 128, n, 4), np.uint8)
        nib[..., 0::2] = words & 0xF
        nib[..., 1::2] = words >> 4
        vals = E2M1[nib]
    vals = vals * np.repeat(np.exp2(scales.astype(np.float64) - 127.0), 8, axis=1)[..., None]
    return vals.transpose(0, 1, 3, 2).reshape(g * 512, n)


def sigmoid(v):
    return 1.0 / (1.0 + np.exp(-v))


K, T, J, R, C, Q, N, S = 512, 1024, 256, 512, 512, 1024, 256, 1024


def setup_inputs():
    n = np.random.standard_normal
    idx = np.random.permutation(T)[:J]
    idx2 = np.random.permutation(C)[:J]
    idx3 = np.random.permutation(C)[:J]
    idx4 = np.random.permutation(Q)[:J]
    idx5 = np.random.permutation(S)[:N]
    fk = mx_kscale(K)
    fr = mx_kscale(R)
    xtp = pack_weight(n((K, T)) / fk[:, None], "e2m1")
    wp = pack_weight(n((K, R)) * 1 / np.sqrt(K) * fk[:, None] * fr, "e5m2")
    w2p = pack_weight(n((K, R)) * 1 / np.sqrt(K) * fk[:, None] * fr, "e4m3")
    vsp = pack_weight(n((R, S)) * 1 / np.sqrt(R) / fr[:, None], "e4m3")
    return {
        "xt_words": xtp[0],
        "xt_scales": xtp[1],
        "w_words": wp[0],
        "w_scales": wp[1],
        "w2_words": w2p[0],
        "w2_scales": w2p[1],
        "tg": (1.0 * n((R, Q))).astype(np.float32),
        "sg": (np.random.uniform(0.6, 1.6, (R, 1))).astype(np.float32),
        "bg": (np.random.uniform(-1.0, 1.0, (R, 1))).astype(np.float32),
        "vs_words": vsp[0],
        "vs_scales": vsp[1],
        "offs": striped(idx),
        "offs2": striped(idx2),
        "offs3": striped(idx3),
        "offs4": striped(idx4),
        "offs5": striped(idx5),
    }


def reference(xt_words, xt_scales, w_words, w_scales, w2_words, w2_scales, tg, sg, bg, vs_words, vs_scales, offs, offs2, offs3, offs4, offs5):
    idx = unstriped(offs)
    idx2 = unstriped(offs2)
    idx3 = unstriped(offs3)
    idx4 = unstriped(offs4)
    idx5 = unstriped(offs5)
    xtu = unpack_weight(xt_words, xt_scales, "e2m1")
    wu = unpack_weight(w_words, w_scales, "e5m2")
    w2u = unpack_weight(w2_words, w2_scales, "e4m3")
    vsu = unpack_weight(vs_words, vs_scales, "e4m3")
    xtidxg = xtu[:, idx]
    a = wu.T @ xtidxg
    b = w2u.T @ xtidxg
    pw = np.zeros((R, C))
    pw[:, idx2] = a
    hid = np.maximum(pw[:, idx3], b) * sigmoid(f64(tg)[:, idx4] * f64(sg) + f64(bg))
    vsidx5g = vsu[:, idx5]
    hidq = mxq(hid, 0, "e5m2")
    y = vsidx5g.T @ hidq
    return y

@@ -1,0 +1,182 @@
+from contextlib import ExitStack
+
+import concourse.mybir as mybir
+
+F32 = mybir.dt.float32
+BF16 = mybir.dt.bfloat16
+I32 = mybir.dt.int32
+U32 = mybir.dt.uint32
+U16 = mybir.dt.uint16
+U8 = mybir.dt.uint8
+E4M3X4 = mybir.dt.float8_e4m3fn_x4
+E5M2X4 = mybir.dt.float8_e5m2_x4
+E2M1X4 = mybir.dt.float4_e2m1fn_x4
+ACT = mybir.ActivationFunctionType
+ALU = mybir.AluOpType
+
+P = 128
+PACK = 4
+T, J, R, C, Q, N, S = 1024, 256, 512, 512, 1024, 256, 1024
+
+FLOPS = 335544320
+
+
+def tile_list_boardtable_twow_store_plain_kernel(
+    tc, xt_words, xt_scales, w_words, w_scales, w2_words, w2_scales, tg, sg, bg,
+    vs_words, vs_scales, offs, offs2, offs3, offs4, offs5, out,
+):
+    nc = tc.nc
+    with ExitStack() as ctx:
+        keep = ctx.enter_context(tc.tile_pool(name="keep", bufs=1))
+        psum = ctx.enter_context(tc.psum_pool(name="psum", bufs=1))
+
+        def load_list(src, name):
+            dst = keep.tile([P, J // 16], U16, name=name)
+            nc.sync.dma_start(dst[:], src)
+            return dst
+
+        def scale_tile(width, name):
+            dst = keep.tile([P, width], U8, name=name, align_bytes=64)
+            nc.vector.memset(dst[:].bitcast(I32), 0)
+            return dst
+
+        def load_scales(queue, dst, src):
+            for q in range(4):
+                queue.dma_start(dst[32 * q : 32 * q + 4, :].bitcast(I32), src[0, 4 * q : 4 * q + 4, :].bitcast(I32))
+
+        def load_words(queue, src, width, name):
+            dst = keep.tile([P, width], U32, name=name, align_bytes=64)
+            queue.dma_start(dst[:].bitcast(I32), src[0].rearrange("p n t -> p (n t)").bitcast(I32))
+            return dst
+
+        def deal(copy, src, dtype, name):
+            dst = keep.tile([P, R], dtype, name=name, align_bytes=64)
+            copy(out=dst[:].rearrange("p (t m) -> p m t", t=PACK), in_=src[:].rearrange("p (m t) -> p m t", t=PACK))
+            return dst
+
+        xs = scale_tile(T, "xs")
+        ws = scale_tile(R, "ws")
+        w2s = scale_tile(R, "w2s")
+        vss = scale_tile(S, "vss")
+        boards = [keep.tile([P, C], F32, name="board%d" % t) for t in range(PACK)]
+        for t in range(PACK):
+            nc.vector.memset(boards[t][:], 0.0)
+
+        idx = load_list(offs, "idx")
+        xw = keep.tile([P, T], U16, name="xw", align_bytes=64)
+        nc.sync.dma_start(xw[:].bitcast(I32), xt_words[0].bitcast(I32))
+        load_scales(nc.sync, xs, xt_scales)
+        ww = load_words(nc.sync, w_words, R, "ww")
+        load_scales(nc.sync, ws, w_scales)
+        idx2 = load_list(offs2, "idx2")
+        idx3 = load_list(offs3, "idx3")
+        w2w = load_words(nc.sync, w2_words, R, "w2w")
+        load_scales(nc.gpsimd, w2s, w2_scales)
+        slope = keep.tile([P, PACK], F32, name="slope")
+        nc.gpsimd.dma_start(slope[:], sg.rearrange("(p t) o -> p (t o)", t=PACK))
+        shift = keep.tile([P, PACK], F32, name="shift")
+        nc.gpsimd.dma_start(shift[:], bg.rearrange("(p t) o -> p (t o)", t=PACK))
+        idx5 = load_list(offs5, "idx5")
+        load_scales(nc.sync, vss, vs_scales)
+        vw = load_words(nc.sync, vs_words, S, "vw")
+        idx4 = load_list(offs4, "idx4")
+        tg_rows = tg.rearrange("(p t) q -> p t q", t=PACK)
+        tables = [keep.tile([P, Q], F32, name="table%d" % t) for t in range(PACK)]
+        for t in range(PACK):
+            nc.sync.dma_start(tables[t][:], tg_rows[:, t, :])
+
+        xgw = keep.tile([P, J], U16, name="xgw", align_bytes=64)
+        nc.vector.tensor_copy(xgw[:], xw[:].indirect(idx[:]))
+        xgs = keep.tile([P, J], U8, name="xgs", align_bytes=64)
+        nc.vector.tensor_copy(xgs[:], xs[:].indirect(idx[:]))
+        wd = deal(nc.scalar.copy, ww, U32, "wd")
+        wsd = deal(nc.vector.tensor_copy, ws, U8, "wsd")
+        w2d = deal(nc.scalar.copy, w2w, U32, "w2d")
+        w2sd = deal(nc.vector.tensor_copy, w2s, U8, "w2sd")
+
+        a_ps = [psum.tile([P, J], F32, name="a_ps%d" % t) for t in range(PACK)]
+        for t in range(PACK):
+            cols = slice(t * P, (t + 1) * P)
+            nc.tensor.matmul_mx(
+                out=a_ps[t][:], lhsT=wd[:, cols].bitcast(E5M2X4), lhsT_scale=wsd[:, cols],
+                rhs=xgw[:].bitcast(E2M1X4), rhs_scale=xgs[:], start=True, stop=True,
+            )
+        b_ps = [psum.tile([P, 2, J], F32, name="b_ps%d" % u) for u in range(2)]
+        for t in range(PACK):
+            cols = slice(t * P, (t + 1) * P)
+            nc.tensor.matmul_mx(
+                out=b_ps[t // 2][:, t % 2, :], lhsT=w2d[:, cols].bitcast(E4M3X4), lhsT_scale=w2sd[:, cols],
+                rhs=xgw[:].bitcast(E2M1X4), rhs_scale=xgs[:], start=True, stop=True,
+            )
+
+        a_sb = [keep.tile([P, J], F32, name="a_sb%d" % t) for t in range(PACK)]
+        picked = [keep.tile([P, J], F32, name="picked%d" % t) for t in range(PACK)]
+        larger = keep.tile([P, PACK, J], F32, name="larger")
+        gate = keep.tile([P, PACK, J], F32, name="gate")
+
+        def scatter(on_vector, t):
+            if on_vector:
+                nc.vector.tensor_copy(boards[t][:].indirect(idx2[:]), a_sb[t][:])
+            else:
+                nc.scalar.activation(boards[t][:].indirect(idx2[:]), a_sb[t][:], ACT.Copy)
+
+        def gather(on_vector, t):
+            if on_vector:
+                nc.vector.tensor_copy(picked[t][:], boards[t][:].indirect(idx3[:]))
+            else:
+                nc.scalar.activation(picked[t][:], boards[t][:].indirect(idx3[:]), ACT.Copy)
+
+        def take_larger(t):
+            nc.vector.tensor_tensor(larger[:, t, :], b_ps[t // 2][:, t % 2, :], picked[t][:], ALU.max)
+
+        def look(t):
+            nc.scalar.activation(
+                out=gate[:, t, :], in_=tables[t][:].indirect(idx4[:]), func=ACT.Sigmoid,
+                bias=shift[:, t : t + 1], scale=slope[:, t : t + 1],
+            )
+
+        nc.vector.tensor_copy(a_sb[0][:], a_ps[0][:])
+        for t in range(1, PACK):
+            nc.scalar.copy(a_sb[t][:], a_ps[t][:])
+        scatter(True, 0)
+        scatter(False, 1)
+        scatter(True, 2)
+        scatter(False, 3)
+        gather(True, 0)
+        gather(False, 1)
+        gather(True, 2)
+        gather(False, 3)
+        vgw = keep.tile([P, N], U32, name="vgw", align_bytes=64)
+        nc.vector.tensor_copy(vgw[:], vw[:].indirect(idx5[:]))
+        vgs = keep.tile([P, N], U8, name="vgs", align_bytes=64)
+        nc.vector.tensor_copy(vgs[:], vss[:].indirect(idx5[:]))
+        for t in range(PACK):
+            take_larger(t)
+        for t in range(PACK):
+            look(t)
+
+        hid = keep.tile([P, J, PACK], BF16, name="hid", align_bytes=64)
+        nc.vector.tensor_tensor(
+            hid[:].rearrange("p (c i) t -> p c t i", i=4),
+            larger[:].rearrange("p t (c i) -> p c t i", i=4),
+            gate[:].rearrange("p t (c i) -> p c t i", i=4),
+            ALU.mult,
+        )
+        hw = keep.tile([P, J], U32, name="hw", align_bytes=64)
+        hs = keep.tile([P, J], U8, name="hs", align_bytes=64)
+        nc.vector.quantize_mx(out=hw[:].bitcast(E5M2X4), scales=hs[:], in_=hid[:].rearrange("p j t -> p (j t)"))
+
+        for h in range(2):
+            cols = slice(h * P, (h + 1) * P)
+            y_ps = psum.tile([P, J], F32, name="y_ps%d" % h)
+            nc.tensor.matmul_mx(
+                out=y_ps[:], lhsT=vgw[:, cols].bitcast(E4M3X4), lhsT_scale=vgs[:, cols],
+                rhs=hw[:].bitcast(E5M2X4), rhs_scale=hs[:], start=True, stop=True,
+            )
+            y_sb = keep.tile([P, J], F32, name="y_sb%d" % h)
+            if h == 0:
+                nc.scalar.copy(y_sb[:], y_ps[:])
+                nc.scalar.dma_start(out[cols, :], y_sb[:])
+            else:
+                nc.vector.tensor_copy(y_sb[:], y_ps[:])
+                nc.sync.dma_start(out[cols, :], y_sb[:])

@@ -35,14 +35,15 @@ def tile_list_boardtable_twow_store_plain_kernel(
             nc.sync.dma_start(dst[:], src)
             return dst
 
-        def scale_tile(width, name):
-            dst = keep.tile([P, width], U8, name=name, align_bytes=64)
-            nc.vector.memset(dst[:].bitcast(I32), 0)
-            return dst
+        def load_scales(queue, dst, src, quadrants):
+            width = dst.shape[1] // 4
+            for q in quadrants:
+                rows = src[0, 4 * q : 4 * q + 4, :].bitcast(I32)
+                queue.dma_start(dst[32 * q : 32 * q + 32, :].bitcast(I32), rows.unsqueeze(0).broadcast_to([8, 4, width]))
 
-        def load_scales(queue, dst, src):
+        def load_scale_rows(dst, src):
             for q in range(4):
-                queue.dma_start(dst[32 * q : 32 * q + 4, :].bitcast(I32), src[0, 4 * q : 4 * q + 4, :].bitcast(I32))
+                nc.sync.dma_start(dst[32 * q : 32 * q + 4, :].bitcast(I32), src[0, 4 * q : 4 * q + 4, :].bitcast(I32))
 
         def load_words(queue, src, width, name):
             dst = keep.tile([P, width], U32, name=name, align_bytes=64)
@@ -54,63 +55,78 @@ def tile_list_boardtable_twow_store_plain_kernel(
             copy(out=dst[:].rearrange("p (t m) -> p m t", t=PACK), in_=src[:].rearrange("p (m t) -> p m t", t=PACK))
             return dst
 
-        xs = scale_tile(T, "xs")
-        ws = scale_tile(R, "ws")
-        w2s = scale_tile(R, "w2s")
-        vss = scale_tile(S, "vss")
+        def deal_by_slot(copy, src, dtype, name, order=(0, 1, 2, 3)):
+            dst = [keep.tile([P, P], dtype, name="%s%d" % (name, t), align_bytes=64) for t in range(PACK)]
+            for t in order:
+                copy(out=dst[t][:], in_=src[:].rearrange("p (m t) -> p t m", t=PACK)[:, t, :])
+            return dst
+
+        tg_rows = tg.rearrange("(p t) q -> p t q", t=PACK)
+        tables = [keep.tile([P, Q], F32, name="table%d" % t) for t in range(PACK)]
+        xs = keep.tile([P, T], U8, name="xs", align_bytes=64)
+        ws = keep.tile([P, R], U8, name="ws", align_bytes=64)
+        w2s = keep.tile([P, R], U8, name="w2s", align_bytes=64)
+        vss = keep.tile([P, S], U8, name="vss", align_bytes=64)
+        nc.vector.memset(w2s[:].bitcast(I32), 0)
+        nc.vector.memset(vss[:].bitcast(I32), 0)
         boards = [keep.tile([P, C], F32, name="board%d" % t) for t in range(PACK)]
         for t in range(PACK):
             nc.vector.memset(boards[t][:], 0.0)
 
-        idx = load_list(offs, "idx")
-        xw = keep.tile([P, T], U16, name="xw", align_bytes=64)
-        nc.sync.dma_start(xw[:].bitcast(I32), xt_words[0].bitcast(I32))
-        load_scales(nc.sync, xs, xt_scales)
-        ww = load_words(nc.sync, w_words, R, "ww")
-        load_scales(nc.sync, ws, w_scales)
-        idx2 = load_list(offs2, "idx2")
-        idx3 = load_list(offs3, "idx3")
-        w2w = load_words(nc.sync, w2_words, R, "w2w")
-        load_scales(nc.gpsimd, w2s, w2_scales)
         slope = keep.tile([P, PACK], F32, name="slope")
         nc.gpsimd.dma_start(slope[:], sg.rearrange("(p t) o -> p (t o)", t=PACK))
         shift = keep.tile([P, PACK], F32, name="shift")
         nc.gpsimd.dma_start(shift[:], bg.rearrange("(p t) o -> p (t o)", t=PACK))
-        idx5 = load_list(offs5, "idx5")
-        load_scales(nc.sync, vss, vs_scales)
-        vw = load_words(nc.sync, vs_words, S, "vw")
-        idx4 = load_list(offs4, "idx4")
-        tg_rows = tg.rearrange("(p t) q -> p t q", t=PACK)
-        tables = [keep.tile([P, Q], F32, name="table%d" % t) for t in range(PACK)]
-        for t in range(PACK):
+
+        idx = load_list(offs, "idx")
+        load_scales(nc.sync, xs, xt_scales, range(4))
+        load_scales(nc.sync, ws, w_scales, range(1))
+        xw = keep.tile([P, T], U16, name="xw", align_bytes=64)
+        nc.sync.dma_start(xw[:].bitcast(I32), xt_words[0].bitcast(I32))
+        ww = load_words(nc.sync, w_words, R, "ww")
+
+        load_scales(nc.sync, ws, w_scales, range(1, 4))
+        idx2 = load_list(offs2, "idx2")
+        idx3 = load_list(offs3, "idx3")
+        w2w = load_words(nc.sync, w2_words, R, "w2w")
+        for t in (0, 1):
             nc.sync.dma_start(tables[t][:], tg_rows[:, t, :])
+
+        load_scale_rows(w2s, w2_scales)
+        idx4 = load_list(offs4, "idx4")
+        vw = load_words(nc.sync, vs_words, S, "vw")
+        nc.sync.dma_start(tables[2][:], tg_rows[:, 2, :])
+        idx5 = load_list(offs5, "idx5")
+
+        load_scale_rows(vss, vs_scales)
+        nc.sync.dma_start(tables[3][:], tg_rows[:, 3, :])
 
         xgw = keep.tile([P, J], U16, name="xgw", align_bytes=64)
         nc.vector.tensor_copy(xgw[:], xw[:].indirect(idx[:]))
         xgs = keep.tile([P, J], U8, name="xgs", align_bytes=64)
         nc.vector.tensor_copy(xgs[:], xs[:].indirect(idx[:]))
         wd = deal(nc.scalar.copy, ww, U32, "wd")
-        wsd = deal(nc.vector.tensor_copy, ws, U8, "wsd")
-        w2d = deal(nc.scalar.copy, w2w, U32, "w2d")
-        w2sd = deal(nc.vector.tensor_copy, w2s, U8, "w2sd")
+        wsd = deal_by_slot(nc.vector.tensor_copy, ws, U8, "wsd", (2, 0, 3, 1))
+        w2d = deal_by_slot(nc.gpsimd.tensor_copy, w2w, U32, "w2d")
+        w2sd = deal_by_slot(nc.gpsimd.tensor_copy, w2s, U8, "w2sd")
 
         a_ps = [psum.tile([P, J], F32, name="a_ps%d" % t) for t in range(PACK)]
-        for t in range(PACK):
+        for t in (2, 0, 3, 1):
             cols = slice(t * P, (t + 1) * P)
             nc.tensor.matmul_mx(
-                out=a_ps[t][:], lhsT=wd[:, cols].bitcast(E5M2X4), lhsT_scale=wsd[:, cols],
+                out=a_ps[t][:], lhsT=wd[:, cols].bitcast(E5M2X4), lhsT_scale=wsd[t][:],
                 rhs=xgw[:].bitcast(E2M1X4), rhs_scale=xgs[:], start=True, stop=True,
             )
         b_ps = [psum.tile([P, 2, J], F32, name="b_ps%d" % u) for u in range(2)]
         for t in range(PACK):
             cols = slice(t * P, (t + 1) * P)
             nc.tensor.matmul_mx(
-                out=b_ps[t // 2][:, t % 2, :], lhsT=w2d[:, cols].bitcast(E4M3X4), lhsT_scale=w2sd[:, cols],
+                out=b_ps[t // 2][:, t % 2, :], lhsT=w2d[t][:].bitcast(E4M3X4), lhsT_scale=w2sd[t][:],
                 rhs=xgw[:].bitcast(E2M1X4), rhs_scale=xgs[:], start=True, stop=True,
             )
 
         a_sb = [keep.tile([P, J], F32, name="a_sb%d" % t) for t in range(PACK)]
-        picked = [keep.tile([P, J], F32, name="picked%d" % t) for t in range(PACK)]
+        picked = [keep.tile([P, 2, J], F32, name="picked%d" % u) for u in range(2)]
         larger = keep.tile([P, PACK, J], F32, name="larger")
         gate = keep.tile([P, PACK, J], F32, name="gate")
 
@@ -122,12 +138,12 @@ def tile_list_boardtable_twow_store_plain_kernel(
 
         def gather(on_vector, t):
             if on_vector:
-                nc.vector.tensor_copy(picked[t][:], boards[t][:].indirect(idx3[:]))
+                nc.vector.tensor_copy(picked[t // 2][:, t % 2, :], boards[t][:].indirect(idx3[:]))
             else:
-                nc.scalar.activation(picked[t][:], boards[t][:].indirect(idx3[:]), ACT.Copy)
+                nc.scalar.activation(picked[t // 2][:, t % 2, :], boards[t][:].indirect(idx3[:]), ACT.Copy)
 
-        def take_larger(t):
-            nc.vector.tensor_tensor(larger[:, t, :], b_ps[t // 2][:, t % 2, :], picked[t][:], ALU.max)
+        def take_larger(u):
+            nc.vector.tensor_tensor(larger[:, 2 * u : 2 * u + 2, :], b_ps[u][:], picked[u][:], ALU.max)
 
         def look(t):
             nc.scalar.activation(
@@ -135,48 +151,52 @@ def tile_list_boardtable_twow_store_plain_kernel(
                 bias=shift[:, t : t + 1], scale=slope[:, t : t + 1],
             )
 
-        nc.vector.tensor_copy(a_sb[0][:], a_ps[0][:])
-        for t in range(1, PACK):
-            nc.scalar.copy(a_sb[t][:], a_ps[t][:])
-        scatter(True, 0)
-        scatter(False, 1)
-        scatter(True, 2)
-        scatter(False, 3)
-        gather(True, 0)
-        gather(False, 1)
-        gather(True, 2)
-        gather(False, 3)
+        for t in (0, 1):
+            nc.vector.tensor_copy(a_sb[t][:], a_ps[t][:])
+            nc.scalar.copy(a_sb[t + 2][:], a_ps[t + 2][:])
+        for t in (0, 1):
+            scatter(True, t)
+            scatter(False, t + 2)
+        for t in (0, 1):
+            gather(True, t)
+            gather(False, t + 2)
+        take_larger(0)
         vgw = keep.tile([P, N], U32, name="vgw", align_bytes=64)
         nc.vector.tensor_copy(vgw[:], vw[:].indirect(idx5[:]))
         vgs = keep.tile([P, N], U8, name="vgs", align_bytes=64)
         nc.vector.tensor_copy(vgs[:], vss[:].indirect(idx5[:]))
-        for t in range(PACK):
-            take_larger(t)
+        take_larger(1)
         for t in range(PACK):
             look(t)
 
-        hid = keep.tile([P, J, PACK], BF16, name="hid", align_bytes=64)
-        nc.vector.tensor_tensor(
-            hid[:].rearrange("p (c i) t -> p c t i", i=4),
-            larger[:].rearrange("p t (c i) -> p c t i", i=4),
-            gate[:].rearrange("p t (c i) -> p c t i", i=4),
-            ALU.mult,
-        )
-        hw = keep.tile([P, J], U32, name="hw", align_bytes=64)
-        hs = keep.tile([P, J], U8, name="hs", align_bytes=64)
-        nc.vector.quantize_mx(out=hw[:].bitcast(E5M2X4), scales=hs[:], in_=hid[:].rearrange("p j t -> p (j t)"))
-
-        for h in range(2):
-            cols = slice(h * P, (h + 1) * P)
-            y_ps = psum.tile([P, J], F32, name="y_ps%d" % h)
-            nc.tensor.matmul_mx(
-                out=y_ps[:], lhsT=vgw[:, cols].bitcast(E4M3X4), lhsT_scale=vgs[:, cols],
-                rhs=hw[:].bitcast(E5M2X4), rhs_scale=hs[:], start=True, stop=True,
+        hid = [keep.tile([P, P, PACK], BF16, name="hid%d" % u, align_bytes=64) for u in range(2)]
+        for u in range(2):
+            slots = slice(u * P, (u + 1) * P)
+            nc.vector.tensor_tensor(
+                hid[u][:].rearrange("p (c i) t -> p c t i", i=4),
+                larger[:, :, slots].rearrange("p t (c i) -> p c t i", i=4),
+                gate[:, :, slots].rearrange("p t (c i) -> p c t i", i=4),
+                ALU.mult,
             )
-            y_sb = keep.tile([P, J], F32, name="y_sb%d" % h)
-            if h == 0:
+        hw = [keep.tile([P, P], U32, name="hw%d" % u, align_bytes=64) for u in range(2)]
+        hs = [keep.tile([P, P], U8, name="hs%d" % u, align_bytes=64) for u in range(2)]
+        for u in range(2):
+            nc.vector.quantize_mx(out=hw[u][:].bitcast(E5M2X4), scales=hs[u][:], in_=hid[u][:].rearrange("p j t -> p (j t)"))
+
+        out_rows = out.rearrange("(h p) j -> p h j", p=P)
+        for u in range(2):
+            slots = slice(u * P, (u + 1) * P)
+            y_ps = psum.tile([P, 2, P], F32, name="y_ps%d" % u)
+            for h in range(2):
+                cols = slice(h * P, (h + 1) * P)
+                nc.tensor.matmul_mx(
+                    out=y_ps[:, h, :], lhsT=vgw[:, cols].bitcast(E4M3X4), lhsT_scale=vgs[:, cols],
+                    rhs=hw[u][:].bitcast(E5M2X4), rhs_scale=hs[u][:], start=True, stop=True,
+                )
+            y_sb = keep.tile([P, 2, P], F32, name="y_sb%d" % u)
+            if u == 0:
                 nc.scalar.copy(y_sb[:], y_ps[:])
-                nc.scalar.dma_start(out[cols, :], y_sb[:])
+                nc.scalar.dma_start(out_rows[:, :, slots], y_sb[:])
             else:
                 nc.vector.tensor_copy(y_sb[:], y_ps[:])
-                nc.sync.dma_start(out[cols, :], y_sb[:])
+                nc.sync.dma_start(out_rows[:, :, slots], y_sb[:])

@@ -15,8 +15,15 @@ ACT = mybir.ActivationFunctionType
 ALU = mybir.AluOpType
 
 P = 128
-PACK = 4
+LANES = 4
+QUADRANTS = 4
+LINE = 4
+HALVES = 2
 T, J, R, C, Q, N, S = 1024, 256, 512, 512, 1024, 256, 1024
+
+VECTOR_LANES = (0, 1)
+SCALAR_LANES = (2, 3)
+LANE_ORDER = (SCALAR_LANES[0], VECTOR_LANES[0], SCALAR_LANES[1], VECTOR_LANES[1])
 
 FLOPS = 335544320
 
@@ -35,168 +42,157 @@ def tile_list_boardtable_twow_store_plain_kernel(
             nc.sync.dma_start(dst[:], src)
             return dst
 
-        def load_scales(queue, dst, src, quadrants):
-            width = dst.shape[1] // 4
-            for q in quadrants:
-                rows = src[0, 4 * q : 4 * q + 4, :].bitcast(I32)
-                queue.dma_start(dst[32 * q : 32 * q + 32, :].bitcast(I32), rows.unsqueeze(0).broadcast_to([8, 4, width]))
-
         def load_scale_rows(dst, src):
-            for q in range(4):
+            for q in range(QUADRANTS):
                 nc.sync.dma_start(dst[32 * q : 32 * q + 4, :].bitcast(I32), src[0, 4 * q : 4 * q + 4, :].bitcast(I32))
 
-        def load_words(queue, src, width, name):
+        def load_fp8_words(src, width, name):
             dst = keep.tile([P, width], U32, name=name, align_bytes=64)
-            queue.dma_start(dst[:].bitcast(I32), src[0].rearrange("p n t -> p (n t)").bitcast(I32))
+            nc.sync.dma_start(dst[:].bitcast(I32), src[0].rearrange("p n t -> p (n t)").bitcast(I32))
             return dst
 
-        def deal(copy, src, dtype, name):
-            dst = keep.tile([P, R], dtype, name=name, align_bytes=64)
-            copy(out=dst[:].rearrange("p (t m) -> p m t", t=PACK), in_=src[:].rearrange("p (m t) -> p m t", t=PACK))
+        def deal_lane_by_lane(copy, src, dtype, name):
+            dst = [keep.tile([P, P], dtype, name="%s%d" % (name, t), align_bytes=64) for t in range(LANES)]
+            for t in LANE_ORDER:
+                copy(out=dst[t][:], in_=src[:].rearrange("p (m t) -> p t m", t=LANES)[:, t, :])
             return dst
 
-        def deal_by_slot(copy, src, dtype, name, order=(0, 1, 2, 3)):
-            dst = [keep.tile([P, P], dtype, name="%s%d" % (name, t), align_bytes=64) for t in range(PACK)]
-            for t in order:
-                copy(out=dst[t][:], in_=src[:].rearrange("p (m t) -> p t m", t=PACK)[:, t, :])
-            return dst
+        tg_lanes = tg.rearrange("(p t) q -> p t q", t=LANES)
+        tables = [keep.tile([P, Q], F32, name="table%d" % t) for t in range(LANES)]
 
-        tg_rows = tg.rearrange("(p t) q -> p t q", t=PACK)
-        tables = [keep.tile([P, Q], F32, name="table%d" % t) for t in range(PACK)]
         xs = keep.tile([P, T], U8, name="xs", align_bytes=64)
+        ws_rows = keep.tile([P, R], U8, name="ws_rows", align_bytes=64)
         ws = keep.tile([P, R], U8, name="ws", align_bytes=64)
         w2s = keep.tile([P, R], U8, name="w2s", align_bytes=64)
-        vss = keep.tile([P, S], U8, name="vss", align_bytes=64)
-        nc.vector.memset(w2s[:].bitcast(I32), 0)
-        nc.vector.memset(vss[:].bitcast(I32), 0)
-        boards = [keep.tile([P, C], F32, name="board%d" % t) for t in range(PACK)]
-        for t in range(PACK):
+        vss = keep.tile([P, S], U8, name="vss", tag="vss", align_bytes=64)
+        nc.vector.memset(xs[:].bitcast(I32), 0)
+
+        warm = keep.tile([P, 2], F32, name="warm")
+        nc.vector.memset(warm[:, 0:1], 0.0)
+        nc.scalar.activation(out=warm[:, 1:2], in_=warm[:, 0:1], func=ACT.Sigmoid)
+
+        for plane in (ws, w2s, vss):
+            nc.vector.memset(plane[:].bitcast(I32), 0)
+        boards = [keep.tile([P, C], F32, name="board%d" % t) for t in range(LANES)]
+        for t in range(LANES):
             nc.vector.memset(boards[t][:], 0.0)
 
-        slope = keep.tile([P, PACK], F32, name="slope")
-        nc.gpsimd.dma_start(slope[:], sg.rearrange("(p t) o -> p (t o)", t=PACK))
-        shift = keep.tile([P, PACK], F32, name="shift")
-        nc.gpsimd.dma_start(shift[:], bg.rearrange("(p t) o -> p (t o)", t=PACK))
+        slope = keep.tile([P, LANES], F32, name="slope")
+        nc.gpsimd.dma_start(slope[:], sg.rearrange("(p t) o -> p (t o)", t=LANES))
+        shift = keep.tile([P, LANES], F32, name="shift")
+        nc.gpsimd.dma_start(shift[:], bg.rearrange("(p t) o -> p (t o)", t=LANES))
 
         idx = load_list(offs, "idx")
-        load_scales(nc.sync, xs, xt_scales, range(4))
-        load_scales(nc.sync, ws, w_scales, range(1))
+        load_scale_rows(ws_rows, w_scales)
         xw = keep.tile([P, T], U16, name="xw", align_bytes=64)
         nc.sync.dma_start(xw[:].bitcast(I32), xt_words[0].bitcast(I32))
-        ww = load_words(nc.sync, w_words, R, "ww")
-
-        load_scales(nc.sync, ws, w_scales, range(1, 4))
+        ww = load_fp8_words(w_words, R, "ww")
+        load_scale_rows(xs, xt_scales)
+        w2w = load_fp8_words(w2_words, R, "w2w")
         idx2 = load_list(offs2, "idx2")
+        vw = load_fp8_words(vs_words, S, "vw")
+        nc.sync.dma_start(tables[0][:], tg_lanes[:, 0, :])
         idx3 = load_list(offs3, "idx3")
-        w2w = load_words(nc.sync, w2_words, R, "w2w")
-        for t in (0, 1):
-            nc.sync.dma_start(tables[t][:], tg_rows[:, t, :])
-
         load_scale_rows(w2s, w2_scales)
-        idx4 = load_list(offs4, "idx4")
-        vw = load_words(nc.sync, vs_words, S, "vw")
-        nc.sync.dma_start(tables[2][:], tg_rows[:, 2, :])
+        nc.sync.dma_start(tables[1][:], tg_lanes[:, 1, :])
         idx5 = load_list(offs5, "idx5")
-
+        nc.sync.dma_start(tables[2][:], tg_lanes[:, 2, :])
+        idx4 = load_list(offs4, "idx4")
         load_scale_rows(vss, vs_scales)
-        nc.sync.dma_start(tables[3][:], tg_rows[:, 3, :])
+        nc.sync.dma_start(tables[3][:], tg_lanes[:, 3, :])
+
+        for q in range(QUADRANTS):
+            rows = slice(32 * q, 32 * q + 4)
+            nc.scalar.copy(ws[rows, :].bitcast(U32), ws_rows[rows, :].bitcast(U32))
 
         xgw = keep.tile([P, J], U16, name="xgw", align_bytes=64)
         nc.vector.tensor_copy(xgw[:], xw[:].indirect(idx[:]))
         xgs = keep.tile([P, J], U8, name="xgs", align_bytes=64)
         nc.vector.tensor_copy(xgs[:], xs[:].indirect(idx[:]))
-        wd = deal(nc.scalar.copy, ww, U32, "wd")
-        wsd = deal_by_slot(nc.vector.tensor_copy, ws, U8, "wsd", (2, 0, 3, 1))
-        w2d = deal_by_slot(nc.gpsimd.tensor_copy, w2w, U32, "w2d")
-        w2sd = deal_by_slot(nc.gpsimd.tensor_copy, w2s, U8, "w2sd")
 
-        a_ps = [psum.tile([P, J], F32, name="a_ps%d" % t) for t in range(PACK)]
-        for t in (2, 0, 3, 1):
-            cols = slice(t * P, (t + 1) * P)
+        wd = deal_lane_by_lane(nc.scalar.copy, ww, U32, "wd")
+        wsd = deal_lane_by_lane(nc.vector.tensor_copy, ws, U8, "wsd")
+        w2d = keep.tile([P, R], U32, name="w2d", align_bytes=64)
+        nc.vector.tensor_copy(
+            out=w2d[:].rearrange("p (t c i) -> p c t i", t=LANES, i=LINE),
+            in_=w2w[:].rearrange("p (c i t) -> p c t i", t=LANES, i=LINE),
+        )
+        w2sd = keep.tile([P, R], U8, name="w2sd", align_bytes=64)
+        nc.vector.tensor_copy(
+            out=w2sd[:].rearrange("p (t m) -> p t m", t=LANES),
+            in_=w2s[:].rearrange("p (m t) -> p t m", t=LANES),
+        )
+
+        a_ps = [psum.tile([P, J], F32, name="a_ps%d" % t) for t in range(LANES)]
+        for t in LANE_ORDER:
             nc.tensor.matmul_mx(
-                out=a_ps[t][:], lhsT=wd[:, cols].bitcast(E5M2X4), lhsT_scale=wsd[t][:],
+                out=a_ps[t][:], lhsT=wd[t][:].bitcast(E5M2X4), lhsT_scale=wsd[t][:],
                 rhs=xgw[:].bitcast(E2M1X4), rhs_scale=xgs[:], start=True, stop=True,
             )
-        b_ps = [psum.tile([P, 2, J], F32, name="b_ps%d" % u) for u in range(2)]
-        for t in range(PACK):
-            cols = slice(t * P, (t + 1) * P)
-            nc.tensor.matmul_mx(
-                out=b_ps[t // 2][:, t % 2, :], lhsT=w2d[t][:].bitcast(E4M3X4), lhsT_scale=w2sd[t][:],
-                rhs=xgw[:].bitcast(E2M1X4), rhs_scale=xgs[:], start=True, stop=True,
-            )
+        slot_half = [slice(u * P, (u + 1) * P) for u in range(HALVES)]
+        b_ps = [psum.tile([P, LANES, P], F32, name="b_ps%d" % u) for u in range(HALVES)]
+        for u in range(HALVES):
+            for t in range(LANES):
+                lane_cols = slice(t * P, (t + 1) * P)
+                nc.tensor.matmul_mx(
+                    out=b_ps[u][:, t, :], lhsT=w2d[:, lane_cols].bitcast(E4M3X4), lhsT_scale=w2sd[:, lane_cols],
+                    rhs=xgw[:, slot_half[u]].bitcast(E2M1X4), rhs_scale=xgs[:, slot_half[u]], start=True, stop=True,
+                )
 
-        a_sb = [keep.tile([P, J], F32, name="a_sb%d" % t) for t in range(PACK)]
-        picked = [keep.tile([P, 2, J], F32, name="picked%d" % u) for u in range(2)]
-        larger = keep.tile([P, PACK, J], F32, name="larger")
-        gate = keep.tile([P, PACK, J], F32, name="gate")
+        picked = keep.tile([P, LANES, J], F32, name="picked")
+        gate = keep.tile([P, LANES, J], F32, name="gate")
+        a_sb = [keep.tile([P, J], F32, name="a_sb%d" % t) for t in range(LANES)]
+        for tv, ts in zip(VECTOR_LANES, SCALAR_LANES):
+            nc.vector.tensor_copy(a_sb[tv][:], a_ps[tv][:])
+            nc.scalar.copy(a_sb[ts][:], a_ps[ts][:])
+        for tv, ts in zip(VECTOR_LANES, SCALAR_LANES):
+            nc.vector.tensor_copy(boards[tv][:].indirect(idx2[:]), a_sb[tv][:])
+            nc.scalar.activation(boards[ts][:].indirect(idx2[:]), a_sb[ts][:], ACT.Copy)
+        for tv, ts in zip(VECTOR_LANES, SCALAR_LANES):
+            nc.vector.tensor_copy(picked[:, tv, :], boards[tv][:].indirect(idx3[:]))
+            nc.scalar.activation(picked[:, ts, :], boards[ts][:].indirect(idx3[:]), ACT.Copy)
 
-        def scatter(on_vector, t):
-            if on_vector:
-                nc.vector.tensor_copy(boards[t][:].indirect(idx2[:]), a_sb[t][:])
-            else:
-                nc.scalar.activation(boards[t][:].indirect(idx2[:]), a_sb[t][:], ACT.Copy)
+        vgw = keep.tile([P, N], U32, name="vgw", align_bytes=64)
+        nc.vector.tensor_copy(vgw[:], vw[:].indirect(idx5[:]))
+        vgs = keep.tile([P, N], U8, name="vgs", align_bytes=64)
+        nc.vector.tensor_copy(vgs[:], vss[:].indirect(idx5[:]))
 
-        def gather(on_vector, t):
-            if on_vector:
-                nc.vector.tensor_copy(picked[t // 2][:, t % 2, :], boards[t][:].indirect(idx3[:]))
-            else:
-                nc.scalar.activation(picked[t // 2][:, t % 2, :], boards[t][:].indirect(idx3[:]), ACT.Copy)
+        larger = keep.tile([P, LANES, J], F32, name="larger", tag="vss", align_bytes=64)
+        for u in range(HALVES):
+            nc.vector.tensor_tensor(larger[:, :, slot_half[u]], b_ps[u][:], picked[:, :, slot_half[u]], ALU.max)
 
-        def take_larger(u):
-            nc.vector.tensor_tensor(larger[:, 2 * u : 2 * u + 2, :], b_ps[u][:], picked[u][:], ALU.max)
-
-        def look(t):
+        for t in range(LANES):
             nc.scalar.activation(
                 out=gate[:, t, :], in_=tables[t][:].indirect(idx4[:]), func=ACT.Sigmoid,
                 bias=shift[:, t : t + 1], scale=slope[:, t : t + 1],
             )
 
-        for t in (0, 1):
-            nc.vector.tensor_copy(a_sb[t][:], a_ps[t][:])
-            nc.scalar.copy(a_sb[t + 2][:], a_ps[t + 2][:])
-        for t in (0, 1):
-            scatter(True, t)
-            scatter(False, t + 2)
-        for t in (0, 1):
-            gather(True, t)
-            gather(False, t + 2)
-        take_larger(0)
-        vgw = keep.tile([P, N], U32, name="vgw", align_bytes=64)
-        nc.vector.tensor_copy(vgw[:], vw[:].indirect(idx5[:]))
-        vgs = keep.tile([P, N], U8, name="vgs", align_bytes=64)
-        nc.vector.tensor_copy(vgs[:], vss[:].indirect(idx5[:]))
-        take_larger(1)
-        for t in range(PACK):
-            look(t)
-
-        hid = [keep.tile([P, P, PACK], BF16, name="hid%d" % u, align_bytes=64) for u in range(2)]
-        for u in range(2):
-            slots = slice(u * P, (u + 1) * P)
+        hid = [keep.tile([P, P, LANES], BF16, name="hid%d" % u, align_bytes=64) for u in range(HALVES)]
+        for u in range(HALVES):
             nc.vector.tensor_tensor(
-                hid[u][:].rearrange("p (c i) t -> p c t i", i=4),
-                larger[:, :, slots].rearrange("p t (c i) -> p c t i", i=4),
-                gate[:, :, slots].rearrange("p t (c i) -> p c t i", i=4),
+                hid[u][:].rearrange("p (c i) t -> p c t i", i=LINE),
+                larger[:, :, slot_half[u]].rearrange("p t (c i) -> p c t i", i=LINE),
+                gate[:, :, slot_half[u]].rearrange("p t (c i) -> p c t i", i=LINE),
                 ALU.mult,
             )
-        hw = [keep.tile([P, P], U32, name="hw%d" % u, align_bytes=64) for u in range(2)]
-        hs = [keep.tile([P, P], U8, name="hs%d" % u, align_bytes=64) for u in range(2)]
-        for u in range(2):
-            nc.vector.quantize_mx(out=hw[u][:].bitcast(E5M2X4), scales=hs[u][:], in_=hid[u][:].rearrange("p j t -> p (j t)"))
+        hw = [keep.tile([P, P], U32, name="hw%d" % u, align_bytes=64) for u in range(HALVES)]
+        hs = [keep.tile([P, P], U8, name="hs%d" % u, align_bytes=64) for u in range(HALVES)]
+        for u in range(HALVES):
+            nc.vector.quantize_mx(
+                out=hw[u][:].bitcast(E5M2X4), scales=hs[u][:], in_=hid[u][:].rearrange("p j t -> p (j t)")
+            )
 
         out_rows = out.rearrange("(h p) j -> p h j", p=P)
-        for u in range(2):
-            slots = slice(u * P, (u + 1) * P)
-            y_ps = psum.tile([P, 2, P], F32, name="y_ps%d" % u)
-            for h in range(2):
-                cols = slice(h * P, (h + 1) * P)
+        copy_out = (nc.scalar.copy, nc.vector.tensor_copy)
+        store = (nc.scalar.dma_start, nc.sync.dma_start)
+        for u in range(HALVES):
+            y_ps = psum.tile([P, HALVES, P], F32, name="y_ps%d" % u)
+            for h in range(HALVES):
+                features = slice(h * P, (h + 1) * P)
                 nc.tensor.matmul_mx(
-                    out=y_ps[:, h, :], lhsT=vgw[:, cols].bitcast(E4M3X4), lhsT_scale=vgs[:, cols],
+                    out=y_ps[:, h, :], lhsT=vgw[:, features].bitcast(E4M3X4), lhsT_scale=vgs[:, features],
                     rhs=hw[u][:].bitcast(E5M2X4), rhs_scale=hs[u][:], start=True, stop=True,
                 )
-            y_sb = keep.tile([P, 2, P], F32, name="y_sb%d" % u)
-            if u == 0:
-                nc.scalar.copy(y_sb[:], y_ps[:])
-                nc.scalar.dma_start(out_rows[:, :, slots], y_sb[:])
-            else:
-                nc.vector.tensor_copy(y_sb[:], y_ps[:])
-                nc.sync.dma_start(out_rows[:, :, slots], y_sb[:])
+            y_sb = keep.tile([P, HALVES, P], F32, name="y_sb%d" % u)
+            copy_out[u](y_sb[:], y_ps[:])
+            store[u](out_rows[:, :, slot_half[u]], y_sb[:])

from contextlib import ExitStack

import concourse.mybir as mybir

F32 = mybir.dt.float32
BF16 = mybir.dt.bfloat16
I32 = mybir.dt.int32
U32 = mybir.dt.uint32
U16 = mybir.dt.uint16
U8 = mybir.dt.uint8
E4M3X4 = mybir.dt.float8_e4m3fn_x4
E5M2X4 = mybir.dt.float8_e5m2_x4
E2M1X4 = mybir.dt.float4_e2m1fn_x4
ACT = mybir.ActivationFunctionType
ALU = mybir.AluOpType

P = 128
LANES = 4
QUADRANTS = 4
LINE = 4
HALVES = 2
T, J, R, C, Q, N, S = 1024, 256, 512, 512, 1024, 256, 1024

VECTOR_LANES = (0, 1)
SCALAR_LANES = (2, 3)
LANE_ORDER = (SCALAR_LANES[0], VECTOR_LANES[0], SCALAR_LANES[1], VECTOR_LANES[1])

FLOPS = 335544320


def tile_list_boardtable_twow_store_plain_kernel(
    tc, xt_words, xt_scales, w_words, w_scales, w2_words, w2_scales, tg, sg, bg,
    vs_words, vs_scales, offs, offs2, offs3, offs4, offs5, out,
):
    nc = tc.nc
    with ExitStack() as ctx:
        keep = ctx.enter_context(tc.tile_pool(name="keep", bufs=1))
        psum = ctx.enter_context(tc.psum_pool(name="psum", bufs=1))

        def load_list(src, name):
            dst = keep.tile([P, J // 16], U16, name=name)
            nc.sync.dma_start(dst[:], src)
            return dst

        def load_scale_rows(dst, src):
            for q in range(QUADRANTS):
                nc.sync.dma_start(dst[32 * q : 32 * q + 4, :].bitcast(I32), src[0, 4 * q : 4 * q + 4, :].bitcast(I32))

        def load_fp8_words(src, width, name):
            dst = keep.tile([P, width], U32, name=name, align_bytes=64)
            nc.sync.dma_start(dst[:].bitcast(I32), src[0].rearrange("p n t -> p (n t)").bitcast(I32))
            return dst

        def deal_lane_by_lane(copy, src, dtype, name):
            dst = [keep.tile([P, P], dtype, name="%s%d" % (name, t), align_bytes=64) for t in range(LANES)]
            for t in LANE_ORDER:
                copy(out=dst[t][:], in_=src[:].rearrange("p (m t) -> p t m", t=LANES)[:, t, :])
            return dst

        tg_lanes = tg.rearrange("(p t) q -> p t q", t=LANES)
        tables = [keep.tile([P, Q], F32, name="table%d" % t) for t in range(LANES)]

        xs = keep.tile([P, T], U8, name="xs", align_bytes=64)
        ws_rows = keep.tile([P, R], U8, name="ws_rows", align_bytes=64)
        ws = keep.tile([P, R], U8, name="ws", align_bytes=64)
        w2s = keep.tile([P, R], U8, name="w2s", align_bytes=64)
        vss = keep.tile([P, S], U8, name="vss", tag="vss", align_bytes=64)
        nc.vector.memset(xs[:].bitcast(I32), 0)

        warm = keep.tile([P, 2], F32, name="warm")
        nc.vector.memset(warm[:, 0:1], 0.0)
        nc.scalar.activation(out=warm[:, 1:2], in_=warm[:, 0:1], func=ACT.Sigmoid)

        for plane in (ws, w2s, vss):
            nc.vector.memset(plane[:].bitcast(I32), 0)
        boards = [keep.tile([P, C], F32, name="board%d" % t) for t in range(LANES)]
        for t in range(LANES):
            nc.vector.memset(boards[t][:], 0.0)

        slope = keep.tile([P, LANES], F32, name="slope")
        nc.gpsimd.dma_start(slope[:], sg.rearrange("(p t) o -> p (t o)", t=LANES))
        shift = keep.tile([P, LANES], F32, name="shift")
        nc.gpsimd.dma_start(shift[:], bg.rearrange("(p t) o -> p (t o)", t=LANES))

        idx = load_list(offs, "idx")
        load_scale_rows(ws_rows, w_scales)
        xw = keep.tile([P, T], U16, name="xw", align_bytes=64)
        nc.sync.dma_start(xw[:].bitcast(I32), xt_words[0].bitcast(I32))
        ww = load_fp8_words(w_words, R, "ww")
        load_scale_rows(xs, xt_scales)
        w2w = load_fp8_words(w2_words, R, "w2w")
        idx2 = load_list(offs2, "idx2")
        vw = load_fp8_words(vs_words, S, "vw")
        nc.sync.dma_start(tables[0][:], tg_lanes[:, 0, :])
        idx3 = load_list(offs3, "idx3")
        load_scale_rows(w2s, w2_scales)
        nc.sync.dma_start(tables[1][:], tg_lanes[:, 1, :])
        idx5 = load_list(offs5, "idx5")
        nc.sync.dma_start(tables[2][:], tg_lanes[:, 2, :])
        idx4 = load_list(offs4, "idx4")
        load_scale_rows(vss, vs_scales)
        nc.sync.dma_start(tables[3][:], tg_lanes[:, 3, :])

        for q in range(QUADRANTS):
            rows = slice(32 * q, 32 * q + 4)
            nc.scalar.copy(ws[rows, :].bitcast(U32), ws_rows[rows, :].bitcast(U32))

        xgw = keep.tile([P, J], U16, name="xgw", align_bytes=64)
        nc.vector.tensor_copy(xgw[:], xw[:].indirect(idx[:]))
        xgs = keep.tile([P, J], U8, name="xgs", align_bytes=64)
        nc.vector.tensor_copy(xgs[:], xs[:].indirect(idx[:]))

        wd = deal_lane_by_lane(nc.scalar.copy, ww, U32, "wd")
        wsd = deal_lane_by_lane(nc.vector.tensor_copy, ws, U8, "wsd")
        w2d = keep.tile([P, R], U32, name="w2d", align_bytes=64)
        nc.vector.tensor_copy(
            out=w2d[:].rearrange("p (t c i) -> p c t i", t=LANES, i=LINE),
            in_=w2w[:].rearrange("p (c i t) -> p c t i", t=LANES, i=LINE),
        )
        w2sd = keep.tile([P, R], U8, name="w2sd", align_bytes=64)
        nc.vector.tensor_copy(
            out=w2sd[:].rearrange("p (t m) -> p t m", t=LANES),
            in_=w2s[:].rearrange("p (m t) -> p t m", t=LANES),
        )

        a_ps = [psum.tile([P, J], F32, name="a_ps%d" % t) for t in range(LANES)]
        for t in LANE_ORDER:
            nc.tensor.matmul_mx(
                out=a_ps[t][:], lhsT=wd[t][:].bitcast(E5M2X4), lhsT_scale=wsd[t][:],
                rhs=xgw[:].bitcast(E2M1X4), rhs_scale=xgs[:], start=True, stop=True,
            )
        slot_half = [slice(u * P, (u + 1) * P) for u in range(HALVES)]
        b_ps = [psum.tile([P, LANES, P], F32, name="b_ps%d" % u) for u in range(HALVES)]
        for u in range(HALVES):
            for t in range(LANES):
                lane_cols = slice(t * P, (t + 1) * P)
                nc.tensor.matmul_mx(
                    out=b_ps[u][:, t, :], lhsT=w2d[:, lane_cols].bitcast(E4M3X4), lhsT_scale=w2sd[:, lane_cols],
                    rhs=xgw[:, slot_half[u]].bitcast(E2M1X4), rhs_scale=xgs[:, slot_half[u]], start=True, stop=True,
                )

        picked = keep.tile([P, LANES, J], F32, name="picked")
        gate = keep.tile([P, LANES, J], F32, name="gate")
        a_sb = [keep.tile([P, J], F32, name="a_sb%d" % t) for t in range(LANES)]
        for tv, ts in zip(VECTOR_LANES, SCALAR_LANES):
            nc.vector.tensor_copy(a_sb[tv][:], a_ps[tv][:])
            nc.scalar.copy(a_sb[ts][:], a_ps[ts][:])
        for tv, ts in zip(VECTOR_LANES, SCALAR_LANES):
            nc.vector.tensor_copy(boards[tv][:].indirect(idx2[:]), a_sb[tv][:])
            nc.scalar.activation(boards[ts][:].indirect(idx2[:]), a_sb[ts][:], ACT.Copy)
        for tv, ts in zip(VECTOR_LANES, SCALAR_LANES):
            nc.vector.tensor_copy(picked[:, tv, :], boards[tv][:].indirect(idx3[:]))
            nc.scalar.activation(picked[:, ts, :], boards[ts][:].indirect(idx3[:]), ACT.Copy)

        vgw = keep.tile([P, N], U32, name="vgw", align_bytes=64)
        nc.vector.tensor_copy(vgw[:], vw[:].indirect(idx5[:]))
        vgs = keep.tile([P, N], U8, name="vgs", align_bytes=64)
        nc.vector.tensor_copy(vgs[:], vss[:].indirect(idx5[:]))

        larger = keep.tile([P, LANES, J], F32, name="larger", tag="vss", align_bytes=64)
        for u in range(HALVES):
            nc.vector.tensor_tensor(larger[:, :, slot_half[u]], b_ps[u][:], picked[:, :, slot_half[u]], ALU.max)

        for t in range(LANES):
            nc.scalar.activation(
                out=gate[:, t, :], in_=tables[t][:].indirect(idx4[:]), func=ACT.Sigmoid,
                bias=shift[:, t : t + 1], scale=slope[:, t : t + 1],
            )

        hid = [keep.tile([P, P, LANES], BF16, name="hid%d" % u, align_bytes=64) for u in range(HALVES)]
        for u in range(HALVES):
            nc.vector.tensor_tensor(
                hid[u][:].rearrange("p (c i) t -> p c t i", i=LINE),
                larger[:, :, slot_half[u]].rearrange("p t (c i) -> p c t i", i=LINE),
                gate[:, :, slot_half[u]].rearrange("p t (c i) -> p c t i", i=LINE),
                ALU.mult,
            )
        hw = [keep.tile([P, P], U32, name="hw%d" % u, align_bytes=64) for u in range(HALVES)]
        hs = [keep.tile([P, P], U8, name="hs%d" % u, align_bytes=64) for u in range(HALVES)]
        for u in range(HALVES):
            nc.vector.quantize_mx(
                out=hw[u][:].bitcast(E5M2X4), scales=hs[u][:], in_=hid[u][:].rearrange("p j t -> p (j t)")
            )

        out_rows = out.rearrange("(h p) j -> p h j", p=P)
        copy_out = (nc.scalar.copy, nc.vector.tensor_copy)
        store = (nc.scalar.dma_start, nc.sync.dma_start)
        for u in range(HALVES):
            y_ps = psum.tile([P, HALVES, P], F32, name="y_ps%d" % u)
            for h in range(HALVES):
                features = slice(h * P, (h + 1) * P)
                nc.tensor.matmul_mx(
                    out=y_ps[:, h, :], lhsT=vgw[:, features].bitcast(E4M3X4), lhsT_scale=vgs[:, features],
                    rhs=hw[u][:].bitcast(E5M2X4), rhs_scale=hs[u][:], start=True, stop=True,
                )
            y_sb = keep.tile([P, HALVES, P], F32, name="y_sb%d" % u)
            copy_out[u](y_sb[:], y_ps[:])
            store[u](out_rows[:, :, slot_half[u]], y_sb[:])
